import numpy as np, ml_dtypes
CORES = [10,50,90]
N = 3
TK = 512
D = 128 * N
def setup_inputs(rng):
    return {"x": (rng.standard_normal((N, 128, TK), dtype=np.float32) + 2 * rng.standard_normal((N, 1, TK), dtype=np.float32)).astype(ml_dtypes.bfloat16)}
def reference(x):
    X = x.astype(np.float64)
    m = X.sum(axis=(0, 1)) / D
    return {"y": (X - m).astype(np.float32), "m": np.broadcast_to(m.astype(np.float32), (N, 1, TK))}

@@ -1,0 +1,115 @@
+from concourse.bass import DstId, RemoteDMATransfer
+from concourse.mybir import AluOpType
+
+SCRATCH = {
+    "xs": ("sbuf", [128, 512], "bfloat16"),
+    "ones": ("sbuf", [128, 8], "bfloat16"),
+    "cb": ("sbuf", [128, 4], "float32"),
+    "a": ("sbuf", [128, 4], "float32"),
+    "q": ("sbuf", [128, 24], "float16"),
+    "v": ("sbuf", [128, 129], "float16"),
+    "zd": ("dram", [16512], "float16"),
+    "eye": ("sbuf", [128, 128], "float16"),
+    "z": ("sbuf", [128, 32], "bfloat16"),
+    "orow": ("sbuf", [128, 128], "bfloat16"),
+    "sel": ("sbuf", [128, 512], "float16"),
+    "r": ("sbuf", [128, 128], "float16"),
+    "ys": ("sbuf", [128, 512], "float32"),
+    "ms": ("sbuf", [128, 128], "float32"),
+    "p1": ("psum", [128, 512], "float32"),
+    "psel": ("psum", [128, 512], "float32"),
+    "pr": ("psum", [128, 512], "float32"),
+    "pm0": ("psum", [128, 512], "float32"),
+    "pm1": ("psum", [128, 512], "float32"),
+    "pm2": ("psum", [128, 512], "float32"),
+    "pm3": ("psum", [128, 512], "float32"),
+    "pmr": ("psum", [128, 512], "float32"),
+}
+SEMAPHORES = ["xl", "kv", "kc", "il", "k1", "kz0", "kz", "p1s", "d1", "d2", "ps", "ds", "arr", "sent",
+              "s1", "s2", "s3_0", "s3_1", "s3_2", "s3_3", "s4", "s5", "s6", "sty", "stm"]
+
+
+def rank_program(g, core, T, topo):
+    rank = T.rank_of(core)
+    if rank is None:
+        return
+    S = T.sem
+    V, P, SY, SC = g.vector, g.tensor, g.sync, g.scalar
+    c0 = 8 * rank
+    others = [c for c in T.cores if c != core]
+    others.sort(key=lambda d: 0 if (topo.chip(d) & 1) != (topo.chip(core) & 1) else 1)
+
+    SY.dma_start(T.xs[:], T.x[:]).then_inc(S.xl, 16)
+
+    V.memset(T.v[:, 0:1], 1.0).then_inc(S.kv, 1)
+    V.memset(T.v[:, 1:129], 0.0).then_inc(S.kv, 1)
+    V.memset(T.ones[:, 0:8], 1.0).then_inc(S.k1, 1)
+    V.memset(T.cb[:, :], 1.0 / 384.0).then_inc(S.k1, 1)
+    V.memset(T.z[0:1, 0:32], 0.0).then_inc(S.kz0, 1)
+    V.memset(T.orow[0:1, 0:128], 1.0).then_inc(S.kz, 1)
+    V.wait_ge(S.kz0, 1)
+    V.memset(T.z[0:1, 0:28:4], 1.0).then_inc(S.kz, 1)
+
+    SC.wait_ge(S.kv, 2)
+    SC.dma_start(T.zd[:], T.v[:, :]).then_inc(S.kc, 16)
+    SC.wait_ge(S.kc, 16)
+    SC.dma_start(T.eye[:, :], T.zd[0:16384]).then_inc(S.il, 16)
+
+    P.wait_ge(S.k1, 2)
+    P.wait_ge(S.xl, 16)
+    for j in range(4):
+        P.matmul(T.p1[:, j:j + 1], T.xs[:, 128 * j:128 * (j + 1)], T.ones[:, 0:1],
+                 start=True, stop=True).then_inc(S.p1s, 1)
+    P.wait_ge(S.kz, 2)
+    for j in range(4):
+        off = (4 - j) % 4
+        P.matmul(T.psel[0:24, 128 * j:128 * (j + 1)], T.z[0:1, off:off + 24], T.orow[0:1, 0:128],
+                 start=True, stop=True).then_inc(S.ps, 1)
+
+    V.wait_ge(S.k1, 2)
+    V.wait_ge(S.p1s, 4)
+    V.tensor_tensor(T.a[:, :], T.p1[:, 0:4], T.cb[:, :], AluOpType.mult).then_inc(S.d1, 1)
+    V.tensor_tensor(T.q[:, c0:c0 + 4], T.p1[:, 0:4], T.cb[:, :], AluOpType.mult).then_inc(S.d1, 1)
+    V.wait_ge(S.d1, 2)
+    V.tensor_tensor(T.q[:, c0 + 4:c0 + 8], T.a[:, :], T.q[:, c0:c0 + 4], AluOpType.subtract).then_inc(S.d2, 1)
+
+    g.wait_ge(S.d2, 1)
+    ids = []
+    for d in others:
+        rid, pid, _se = topo.addr(d)
+        ids.append(DstId(rid=rid, pnc=pid))
+    own = T.q[:, c0:c0 + 8]
+    g.remote_dma_fused([RemoteDMATransfer(dst_ids=ids, dma_engine_mask=0xFF, remote_sem=S.arr,
+                                          srcs=[own], dsts=[own, own], alu_op=0)], local_sem=S.sent)
+
+    V.wait_ge(S.ps, 4)
+    V.tensor_copy(T.sel[0:24, :], T.psel[0:24, :]).then_inc(S.ds, 1)
+
+    P.wait_ge(S.il, 16)
+    P.wait_ge(S.d2, 1)
+    P.wait_ge(S.arr, 16)
+    P.matmul(T.pr[0:24, 0:128], T.q[:, 0:24], T.eye[:, :], start=True, stop=True).then_inc(S.s1, 1)
+    V.wait_ge(S.s1, 1)
+    V.tensor_copy(T.r[0:24, :], T.pr[0:24, 0:128]).then_inc(S.s2, 1)
+    P.wait_ge(S.ds, 1)
+    P.wait_ge(S.s2, 1)
+    for j in range(4):
+        P.matmul(T["pm%d" % j][:, 0:128], T.sel[0:24, 128 * j:128 * (j + 1)], T.r[0:24, :],
+                 start=True, stop=True).then_inc(S["s3_%d" % j], 1)
+    P.matmul(T.pmr[0:4, 0:128], T.sel[0:24, 0:512:128], T.r[0:24, :], start=True, stop=True).then_inc(S.s4, 1)
+
+    V.wait_ge(S.xl, 16)
+    for j in range(4):
+        V.wait_ge(S["s3_%d" % j], 1)
+        V.tensor_tensor(T.ys[:, 128 * j:128 * (j + 1)], T.xs[:, 128 * j:128 * (j + 1)], T["pm%d" % j][:, 0:128],
+                        AluOpType.subtract).then_inc(S.s5, 1)
+    V.wait_ge(S.s4, 1)
+    V.tensor_copy(T.ms[0:4, :], T.pmr[0:4, 0:128]).then_inc(S.s6, 1)
+
+    SY.wait_ge(S.s5, 4)
+    SY.dma_start(T.y[:], T.ys[:]).then_inc(S.sty, 16)
+    SC.wait_ge(S.s6, 1)
+    SC.dma_start(T.m[:], T.ms[0:4, :]).then_inc(S.stm, 16)
+    SY.wait_ge(S.sty, 16)
+    SC.wait_ge(S.stm, 16)
+    g.wait_ge(S.sent, 8)

@@ -1,6 +1,8 @@
 from concourse.bass import DstId, RemoteDMATransfer
 from concourse.mybir import AluOpType
 
+YCUTS = [1, 2, 3, 4]
+
 SCRATCH = {
     "xs": ("sbuf", [128, 512], "bfloat16"),
     "ones": ("sbuf", [128, 8], "bfloat16"),
@@ -26,7 +28,8 @@ SCRATCH = {
     "pmr": ("psum", [128, 512], "float32"),
 }
 SEMAPHORES = ["xl", "kv", "kc", "il", "k1", "kz0", "kz", "p1s", "d1", "d2", "ps", "ds", "arr", "sent",
-              "s1", "s2", "s3_0", "s3_1", "s3_2", "s3_3", "s4", "s5", "s6", "sty", "stm"]
+              "s1", "s2", "s3_0", "s3_1", "s3_2", "s3_3", "s4", "s5_0", "s5_1", "s5_2", "s5_3", "s6",
+              "sty", "stc"]
 
 
 def rank_program(g, core, T, topo):
@@ -102,14 +105,23 @@ def rank_program(g, core, T, topo):
     for j in range(4):
         V.wait_ge(S["s3_%d" % j], 1)
         V.tensor_tensor(T.ys[:, 128 * j:128 * (j + 1)], T.xs[:, 128 * j:128 * (j + 1)], T["pm%d" % j][:, 0:128],
-                        AluOpType.subtract).then_inc(S.s5, 1)
+                        AluOpType.subtract).then_inc(S["s5_%d" % j], 1)
     V.wait_ge(S.s4, 1)
     V.tensor_copy(T.ms[0:4, :], T.pmr[0:4, 0:128]).then_inc(S.s6, 1)
 
-    SY.wait_ge(S.s5, 4)
-    SY.dma_start(T.y[:], T.ys[:]).then_inc(S.sty, 16)
-    SC.wait_ge(S.s6, 1)
-    SC.dma_start(T.m[:], T.ms[0:4, :]).then_inc(S.stm, 16)
-    SY.wait_ge(S.sty, 16)
-    SC.wait_ge(S.stm, 16)
+    queues = [(SY, S.sty), (SC, S.stc)]
+    count = [0, 0]
+    lo = 0
+    for i, hi in enumerate(YCUTS):
+        Q, sem = queues[i % 2]
+        for j in range(lo, hi):
+            Q.wait_ge(S["s5_%d" % j], 1)
+        Q.dma_start(T.y[:, 128 * lo:128 * hi], T.ys[:, 128 * lo:128 * hi]).then_inc(sem, 16)
+        count[i % 2] += 16
+        lo = hi
+    SY.wait_ge(S.s6, 1)
+    SY.dma_start(T.m[:], T.ms[0:4, :]).then_inc(S.sty, 16)
+    count[0] += 16
+    SY.wait_ge(S.sty, count[0])
+    SC.wait_ge(S.stc, count[1])
     g.wait_ge(S.sent, 8)

from concourse.bass import DstId, RemoteDMATransfer
from concourse.mybir import AluOpType

YCUTS = [1, 2, 3, 4]

SCRATCH = {
    "xs": ("sbuf", [128, 512], "bfloat16"),
    "ones": ("sbuf", [128, 8], "bfloat16"),
    "cb": ("sbuf", [128, 4], "float32"),
    "a": ("sbuf", [128, 4], "float32"),
    "q": ("sbuf", [128, 24], "float16"),
    "v": ("sbuf", [128, 129], "float16"),
    "zd": ("dram", [16512], "float16"),
    "eye": ("sbuf", [128, 128], "float16"),
    "z": ("sbuf", [128, 32], "bfloat16"),
    "orow": ("sbuf", [128, 128], "bfloat16"),
    "sel": ("sbuf", [128, 512], "float16"),
    "r": ("sbuf", [128, 128], "float16"),
    "ys": ("sbuf", [128, 512], "float32"),
    "ms": ("sbuf", [128, 128], "float32"),
    "p1": ("psum", [128, 512], "float32"),
    "psel": ("psum", [128, 512], "float32"),
    "pr": ("psum", [128, 512], "float32"),
    "pm0": ("psum", [128, 512], "float32"),
    "pm1": ("psum", [128, 512], "float32"),
    "pm2": ("psum", [128, 512], "float32"),
    "pm3": ("psum", [128, 512], "float32"),
    "pmr": ("psum", [128, 512], "float32"),
}
SEMAPHORES = ["xl", "kv", "kc", "il", "k1", "kz0", "kz", "p1s", "d1", "d2", "ps", "ds", "arr", "sent",
              "s1", "s2", "s3_0", "s3_1", "s3_2", "s3_3", "s4", "s5_0", "s5_1", "s5_2", "s5_3", "s6",
              "sty", "stc"]


def rank_program(g, core, T, topo):
    rank = T.rank_of(core)
    if rank is None:
        return
    S = T.sem
    V, P, SY, SC = g.vector, g.tensor, g.sync, g.scalar
    c0 = 8 * rank
    others = [c for c in T.cores if c != core]
    others.sort(key=lambda d: 0 if (topo.chip(d) & 1) != (topo.chip(core) & 1) else 1)

    SY.dma_start(T.xs[:], T.x[:]).then_inc(S.xl, 16)

    V.memset(T.v[:, 0:1], 1.0).then_inc(S.kv, 1)
    V.memset(T.v[:, 1:129], 0.0).then_inc(S.kv, 1)
    V.memset(T.ones[:, 0:8], 1.0).then_inc(S.k1, 1)
    V.memset(T.cb[:, :], 1.0 / 384.0).then_inc(S.k1, 1)
    V.memset(T.z[0:1, 0:32], 0.0).then_inc(S.kz0, 1)
    V.memset(T.orow[0:1, 0:128], 1.0).then_inc(S.kz, 1)
    V.wait_ge(S.kz0, 1)
    V.memset(T.z[0:1, 0:28:4], 1.0).then_inc(S.kz, 1)

    SC.wait_ge(S.kv, 2)
    SC.dma_start(T.zd[:], T.v[:, :]).then_inc(S.kc, 16)
    SC.wait_ge(S.kc, 16)
    SC.dma_start(T.eye[:, :], T.zd[0:16384]).then_inc(S.il, 16)

    P.wait_ge(S.k1, 2)
    P.wait_ge(S.xl, 16)
    for j in range(4):
        P.matmul(T.p1[:, j:j + 1], T.xs[:, 128 * j:128 * (j + 1)], T.ones[:, 0:1],
                 start=True, stop=True).then_inc(S.p1s, 1)
    P.wait_ge(S.kz, 2)
    for j in range(4):
        off = (4 - j) % 4
        P.matmul(T.psel[0:24, 128 * j:128 * (j + 1)], T.z[0:1, off:off + 24], T.orow[0:1, 0:128],
                 start=True, stop=True).then_inc(S.ps, 1)

    V.wait_ge(S.k1, 2)
    V.wait_ge(S.p1s, 4)
    V.tensor_tensor(T.a[:, :], T.p1[:, 0:4], T.cb[:, :], AluOpType.mult).then_inc(S.d1, 1)
    V.tensor_tensor(T.q[:, c0:c0 + 4], T.p1[:, 0:4], T.cb[:, :], AluOpType.mult).then_inc(S.d1, 1)
    V.wait_ge(S.d1, 2)
    V.tensor_tensor(T.q[:, c0 + 4:c0 + 8], T.a[:, :], T.q[:, c0:c0 + 4], AluOpType.subtract).then_inc(S.d2, 1)

    g.wait_ge(S.d2, 1)
    ids = []
    for d in others:
        rid, pid, _se = topo.addr(d)
        ids.append(DstId(rid=rid, pnc=pid))
    own = T.q[:, c0:c0 + 8]
    g.remote_dma_fused([RemoteDMATransfer(dst_ids=ids, dma_engine_mask=0xFF, remote_sem=S.arr,
                                          srcs=[own], dsts=[own, own], alu_op=0)], local_sem=S.sent)

    V.wait_ge(S.ps, 4)
    V.tensor_copy(T.sel[0:24, :], T.psel[0:24, :]).then_inc(S.ds, 1)

    P.wait_ge(S.il, 16)
    P.wait_ge(S.d2, 1)
    P.wait_ge(S.arr, 16)
    P.matmul(T.pr[0:24, 0:128], T.q[:, 0:24], T.eye[:, :], start=True, stop=True).then_inc(S.s1, 1)
    V.wait_ge(S.s1, 1)
    V.tensor_copy(T.r[0:24, :], T.pr[0:24, 0:128]).then_inc(S.s2, 1)
    P.wait_ge(S.ds, 1)
    P.wait_ge(S.s2, 1)
    for j in range(4):
        P.matmul(T["pm%d" % j][:, 0:128], T.sel[0:24, 128 * j:128 * (j + 1)], T.r[0:24, :],
                 start=True, stop=True).then_inc(S["s3_%d" % j], 1)
    P.matmul(T.pmr[0:4, 0:128], T.sel[0:24, 0:512:128], T.r[0:24, :], start=True, stop=True).then_inc(S.s4, 1)

    V.wait_ge(S.xl, 16)
    for j in range(4):
        V.wait_ge(S["s3_%d" % j], 1)
        V.tensor_tensor(T.ys[:, 128 * j:128 * (j + 1)], T.xs[:, 128 * j:128 * (j + 1)], T["pm%d" % j][:, 0:128],
                        AluOpType.subtract).then_inc(S["s5_%d" % j], 1)
    V.wait_ge(S.s4, 1)
    V.tensor_copy(T.ms[0:4, :], T.pmr[0:4, 0:128]).then_inc(S.s6, 1)

    queues = [(SY, S.sty), (SC, S.stc)]
    count = [0, 0]
    lo = 0
    for i, hi in enumerate(YCUTS):
        Q, sem = queues[i % 2]
        for j in range(lo, hi):
            Q.wait_ge(S["s5_%d" % j], 1)
        Q.dma_start(T.y[:, 128 * lo:128 * hi], T.ys[:, 128 * lo:128 * hi]).then_inc(sem, 16)
        count[i % 2] += 16
        lo = hi
    SY.wait_ge(S.s6, 1)
    SY.dma_start(T.m[:], T.ms[0:4, :]).then_inc(S.sty, 16)
    count[0] += 16
    SY.wait_ge(S.sty, count[0])
    SC.wait_ge(S.stc, count[1])
    g.wait_ge(S.sent, 8)
